import numpy as np, ml_dtypes
CORES = [4,20,36,44,92,100,108,116,3,19,35,43,91,99,107,115]
N = 16
TK, LAY = 512, 4
def setup_inputs(rng):
    return {"x": rng.standard_normal((N, 128, TK), dtype=np.float32).astype(ml_dtypes.bfloat16), "wu": (rng.standard_normal((N, 128, LAY * 256), dtype=np.float32) / 16).astype(ml_dtypes.bfloat16), "wd": (rng.standard_normal((N, 128, 256), dtype=np.float32) / 16).astype(ml_dtypes.bfloat16)}
def setup_inputs_big(rng):
    d = setup_inputs(rng)
    for k in ("x",): d[k] = (d[k].astype(np.float32) * 1048576.0).astype(d[k].dtype)
    return d
def setup_inputs_small(rng):
    d = setup_inputs(rng)
    for k in ("x",): d[k] = (d[k].astype(np.float32) * (1 / 1048576.0)).astype(d[k].dtype)
    return d
def setup_inputs_apart(rng):
    d = setup_inputs(rng)
    f = (10.0 ** rng.permutation(np.linspace(-1.5, 1.5, N))).astype(np.float32).reshape(N, 1, 1)
    for k in ("x",): d[k] = (d[k].astype(np.float32) * f).astype(d[k].dtype)
    return d
def reference(x, wu, wd):
    X, WU, WD = x.astype(np.float64), wu.astype(np.float64), wd.astype(np.float64)
    s = list(X)
    for l in range(LAY):
        for q in range(0, N, 2 << l):
            p = q + (1 << l)
            s[q] = np.maximum(WU[q][:, 256 * l:256 * l + 128].T @ s[q] + WU[q][:, 256 * l + 128:256 * l + 256].T @ s[p], 0.0)
    for l in range(LAY - 1, -1, -1):
        for q in range(0, N, 2 << l):
            p = q + (1 << l)
            s[p] = np.maximum(WD[p][:, 0:128].T @ s[p] + WD[p][:, 128:256].T @ s[q], 0.0)
    return {"y": np.stack(s).astype(ml_dtypes.bfloat16)}

@@ -1,0 +1,385 @@
+from concourse.bass import DstId, RemoteDMATransfer
+from concourse.mybir import AluOpType
+
+TK = 512
+NP = 2
+PW = TK // NP
+POOL = 12288
+NM, NL = 44, 52
+
+SCRATCH = {
+    "pool": ("sbuf", [128, POOL], "bfloat16"),
+    "zero": ("sbuf", [128, PW], "float32"),
+}
+for _b in range(8):
+    SCRATCH["ps%d" % _b] = ("psum", [128, 512], "float32")
+SEMAPHORES = ["m%d" % i for i in range(NM)] + ["l%d" % i for i in range(NL)] + ["sent"]
+
+
+def _bits(m):
+    n = 0
+    while m:
+        n += m & 1
+        m >>= 1
+    return n
+
+
+def rank_program(g, core, T, topo):
+    me = core
+    rk = list(T.cores)
+    queues = {"g": g, "t": g.tensor, "v": g.vector, "s": g.sync, "a": g.scalar}
+    nmsg = [0]
+    nloc, ncol, waited, sent, banks, where, zcond = {}, {}, {}, {}, {}, {}, {}
+    seq = [0]
+
+    def lsem(c):
+        n = nloc.get(c, 0)
+        nloc[c] = n + 1
+        assert n < NL
+        return "l%d" % n
+
+    def alloc(c, w):
+        o = ncol.get(c, 0)
+        ncol[c] = o + w
+        assert o + w <= POOL
+        return o
+
+    def wait(c, q, conds):
+        done = waited.setdefault((c, q), set())
+        for cd in conds:
+            if cd not in done:
+                done.add(cd)
+                if c == me:
+                    queues[q].wait_ge(T.sem[cd[0]], cd[1])
+
+    def reg(c, name, off, w, conds):
+        where[(c, name)] = (off, w, [list(conds) for _ in range(NP)])
+
+    def regs(c, off, conds, spec):
+        for name, w in spec:
+            reg(c, name, off, w, conds)
+            off += w
+
+    def allconds(c, name):
+        out = []
+        for pc in where[(c, name)][2]:
+            for cd in pc:
+                if cd not in out:
+                    out.append(cd)
+        return out
+
+    def load(c, q, off, tensor, a, b):
+        s = lsem(c)
+        if c == me:
+            queues[q].dma_start(T.pool[:, off:off + b - a], T[tensor][:, a:b]).then_inc(T.sem[s], 16)
+        return (s, 16)
+
+    def send(src, off, w, conds, dsts):
+        s = "m%d" % nmsg[0]
+        nmsg[0] += 1
+        assert nmsg[0] <= NM
+        wait(src, "g", conds)
+        near = [d for d in dsts if topo.chip(d) == topo.chip(src)]
+        far = [d for d in dsts if topo.chip(d) != topo.chip(src)]
+        groups = []
+        mfar = 0
+        if far:
+            mfar = topo.mask(src, far[0])
+            for d in far:
+                mfar &= topo.mask(src, d)
+            groups.append((far, mfar))
+        if near:
+            mnear = topo.mask(src, near[0])
+            for d in near:
+                mnear &= topo.mask(src, d)
+            groups.append((near, mnear & ~mfar))
+        out = {}
+        trs = []
+        for ds, m in groups:
+            n = _bits(m)
+            assert n in (1, 2, 4, 8, 16)
+            sent[src] = sent.get(src, 0) + n
+            ids, aps = [], []
+            for d in ds:
+                assert topo.may_write(src, d) and d != src
+                o = alloc(d, w)
+                out[d] = (o, (s, n))
+                rid, pid, _se = topo.addr(d)
+                ids.append((rid, pid))
+                aps.append(o)
+            trs.append((ids, aps, m))
+        if src == me:
+            sap = T.pool[:, off:off + w]
+            if len(trs) == 1 and len(trs[0][0]) == 1:
+                (ids, aps, m) = trs[0]
+                g.remote_dma(out_ap=T.pool[:, aps[0]:aps[0] + w], in_ap=sap, remote_sem=T.sem[s],
+                             local_sem=T.sem.sent, pid=ids[0][1], routing_id=ids[0][0], dma_engine_mask=m)
+            else:
+                g.remote_dma_fused(
+                    [RemoteDMATransfer(dst_ids=[DstId(rid=r, pnc=p) for r, p in ids], dma_engine_mask=m,
+                                       remote_sem=T.sem[s], srcs=[sap],
+                                       dsts=[T.pool[:, o:o + w] for o in aps], alu_op=0)
+                     for ids, aps, m in trs],
+                    local_sem=T.sem.sent)
+        return out
+
+    def send_val(src, name, dsts):
+        off, w, _c = where[(src, name)]
+        res = send(src, off, w, allconds(src, name), dsts)
+        for d in dsts:
+            reg(d, name, res[d][0], w, [res[d][1]])
+
+    def zeros(c):
+        if c not in zcond:
+            s = lsem(c)
+            zcond[c] = (s, 1)
+            if c == me:
+                g.vector.memset(T.zero[:], 0.0).then_inc(T.sem[s], 1)
+
+    open_nodes = {}
+
+    def mm(c, node, p, tile, opnd, first, last):
+        zeros(c)
+        bl = banks.setdefault(c, [None] * 8)
+        toff, _tw, tc = where[(c, tile)]
+        ooff, _ow, oc = where[(c, opnd)]
+        conds = list(tc[p]) + list(oc[p])
+        if first:
+            if (c, node) not in open_nodes:
+                open_nodes[(c, node)] = {"off": alloc(c, TK), "bank": [None] * NP, "conds": [None] * NP}
+            free = [b for b in range(8) if bl[b] is None]
+            if free:
+                b = free[0]
+            else:
+                closed = [b for b in range(8) if bl[b][1] is not None]
+                assert closed, "no PSUM bank free"
+                b = min(closed, key=lambda k: bl[k][0])
+                conds.append(bl[b][1])
+            seq[0] += 1
+            bl[b] = [seq[0], None]
+            open_nodes[(c, node)]["bank"][p] = b
+        nd = open_nodes[(c, node)]
+        b = nd["bank"][p]
+        wait(c, "t", conds)
+        ms = lsem(c) if last else None
+        if c == me:
+            ins = g.tensor.matmul(T["ps%d" % b][:, 0:PW], T.pool[:, toff:toff + 128],
+                                  T.pool[:, ooff + p * PW:ooff + (p + 1) * PW], first, last)
+            if last:
+                ins.then_inc(T.sem[ms], 1)
+        if last:
+            rs = lsem(c)
+            wait(c, "v", [zcond[c], (ms, 1)])
+            if c == me:
+                g.vector.tensor_tensor(T.pool[:, nd["off"] + p * PW:nd["off"] + (p + 1) * PW],
+                                       T["ps%d" % b][:, 0:PW], T.zero[:, 0:PW], AluOpType.max).then_inc(T.sem[rs], 1)
+            seq[0] += 1
+            bl[b] = [seq[0], (rs, 1)]
+            nd["conds"][p] = [(rs, 1)]
+            if all(x is not None for x in nd["conds"]):
+                where[(c, node)] = (nd["off"], TK, nd["conds"])
+
+    def start(c, node, tile, opnd):
+        for p in range(NP):
+            mm(c, node, p, tile, opnd, True, False)
+
+    def finish(c, node, tile, opnd):
+        for p in range(NP):
+            mm(c, node, p, tile, opnd, False, True)
+
+    def store(c, name):
+        off, _w, pc = where[(c, name)]
+        if all(x == pc[0] for x in pc):
+            parts = [("s", 0, TK, pc[0])]
+        else:
+            parts = [("sa"[p % 2], p * PW, (p + 1) * PW, pc[p]) for p in range(NP)]
+        for q, a, b, conds in parts:
+            wait(c, q, conds)
+            s = lsem(c)
+            if c == me:
+                queues[q].dma_start(T.y[:, a:b], T.pool[:, off + a:off + b]).then_inc(T.sem[s], 16)
+            wait(c, q, [(s, 16)])
+
+    def reaches_all(c):
+        return all(topo.may_write(c, d) for d in rk if d != c)
+
+    allcores = range(topo.CHIPS * topo.CORES_PER_CHIP)
+
+    def centre_of(r):
+        c = rk[r]
+        if reaches_all(c):
+            return c
+        for h in allcores:
+            if topo.chip(h) == topo.chip(c) and topo.die(h) == topo.die(c) and h not in rk and reaches_all(h):
+                return h
+        raise ValueError("no centre")
+
+    Q = {q: centre_of(q) for q in (0, 4, 8, 12)}
+
+    def relay_for(c, dst):
+        for h in rk:
+            if h != c and topo.chip(h) == topo.chip(c) and h not in Q.values() and topo.may_write(h, dst):
+                return h
+        for h in allcores:
+            if h != c and topo.chip(h) == topo.chip(c) and h not in rk and h not in Q.values() \
+                    and topo.may_write(h, dst):
+                return h
+        raise ValueError("no relay")
+
+    def uv(r, levels):
+        out = []
+        for l in levels:
+            out += [("U%d.%d" % (r, l), 128), ("V%d.%d" % (r, l), 128)]
+        return out
+
+    def de(r):
+        return [("D%d" % r, 128), ("E%d" % r, 128)]
+
+    relays = []
+
+    def to_centre(c, dst, off, w, conds, spec):
+        if c == dst:
+            regs(c, off, conds, spec)
+        elif topo.may_write(c, dst):
+            o, cd = send(c, off, w, conds, [dst])[dst]
+            regs(dst, o, [cd], spec)
+        else:
+            h = relay_for(c, dst)
+            o, cd = send(c, off, w, conds, [h])[h]
+            relays.append((h, dst, o, w, cd, spec))
+
+    top = {}
+    for r in (8, 12, 9, 10, 11, 13, 14, 15, 0, 4, 1, 2, 3, 5, 6, 7):
+        c = rk[r]
+        q = r - r % 4
+        if r % 2:
+            ox, ow = alloc(c, TK), alloc(c, 256)
+            cx = load(c, "s", ox, "x", 0, TK)
+            cw = load(c, "a", ow, "wd", 0, 256)
+            reg(c, "x%d" % r, ox, TK, [cx])
+            regs(c, ow, [cw], de(r))
+            to_centre(c, Q[q], ox, TK, [cx], [("x%d" % r, TK)])
+            start(c, "b%d" % r, "D%d" % r, "x%d" % r)
+        elif r % 4:
+            o = alloc(c, TK + 512)
+            cs = [load(c, "s", o, "x", 0, TK), load(c, "a", o + TK, "wu", 0, 256),
+                  load(c, "a", o + TK + 256, "wd", 0, 256)]
+            to_centre(c, Q[q], o, TK + 512, cs, [("x%d" % r, TK)] + uv(r, [0]) + de(r))
+        else:
+            if r == 0:
+                o = alloc(c, 512)
+                cs = [load(c, "s", o, "wu", 512, 1024)]
+                top[0] = (o, 512, cs, uv(0, [2, 3]))
+                to_centre(c, Q[0], o, 512, cs, uv(0, [2, 3]))
+            if r == 8:
+                o = alloc(c, 512)
+                cs = [load(c, "s", o, "wu", 512, 768), load(c, "a", o + 256, "wd", 0, 256)]
+                to_centre(c, Q[8], o, 512, cs, uv(8, [2]) + de(8))
+            spec = [("x%d" % r, TK)] + uv(r, [0, 1])
+            w = TK + 512
+            o = alloc(c, w + (256 if r % 8 else 0))
+            cs = [load(c, "a" if r == 0 else "s", o, "x", 0, TK), load(c, "s" if r == 0 else "a", o + TK, "wu", 0, 512)]
+            if r % 8:
+                cs.append(load(c, "s", o + w, "wd", 0, 256))
+                spec += de(r)
+                w += 256
+            to_centre(c, Q[q], o, w, cs, spec)
+
+    for h, dst, o, w, cd, spec in relays:
+        o2, cd2 = send(h, o, w, [cd], [dst])[dst]
+        regs(dst, o2, [cd2], spec)
+
+    def spread(src, first_tile, spec, dsts):
+        off = where[(src, first_tile)][0]
+        w = sum(x[1] for x in spec)
+        res = send(src, off, w, allconds(src, first_tile), dsts)
+        for d in dsts:
+            regs(d, res[d][0], [res[d][1]], spec)
+
+    spec8 = uv(8, [2]) + de(8)
+    spread(Q[8], "U8.2", spec8, [Q[0], Q[4]])
+    spread(Q[4], "U8.2", spec8, [Q[12]])
+    spread(Q[0], "U0.2", uv(0, [2, 3]), [Q[8], Q[12], Q[4]])
+
+    for q in (8, 12, 0, 4):
+        c = Q[q]
+        a0, a2, a1 = "a%d.0" % q, "a%d.0" % (q + 2), "a%d.1" % q
+        start(c, a0, "U%d.0" % q, "x%d" % q)
+        start(c, a2, "U%d.0" % (q + 2), "x%d" % (q + 2))
+        finish(c, a0, "V%d.0" % q, "x%d" % (q + 1))
+        start(c, a1, "U%d.1" % q, a0)
+        finish(c, a2, "V%d.0" % (q + 2), "x%d" % (q + 3))
+        finish(c, a1, "V%d.1" % q, a2)
+        others = [Q[o] for o in (12, 8, 4, 0) if o != q]
+        near = [d for d in others if topo.chip(d) == topo.chip(c)]
+        far = [d for d in others if topo.chip(d) != topo.chip(c)]
+        if q >= 8:
+            send_val(c, a1, near + far)
+        else:
+            send_val(c, a1, near + far[:1])
+            for d in far[1:]:
+                send_val(c, a1, [d])
+
+    def near_first(c, terms, src):
+        return sorted(terms, key=lambda t: 0 if topo.chip(Q[src[t[1]]]) == topo.chip(c) else 1)
+
+    for q in (8, 12, 0, 4):
+        c = Q[q]
+        if q == 0:
+            start(c, "b2", "D2", "a2.0")
+        if q == 4:
+            start(c, "b4", "D4", "a4.1")
+            start(c, "b6", "D6", "a6.0")
+        if q == 8:
+            start(c, "b10", "D10", "a10.0")
+        if q == 12:
+            start(c, "b12", "D12", "a12.1")
+        t = near_first(c, [("U8.2", "a8.1"), ("V8.2", "a12.1")], {"a8.1": 8, "a12.1": 12})
+        start(c, "a8.2", t[0][0], t[0][1])
+        finish(c, "a8.2", t[1][0], t[1][1])
+        if q >= 8:
+            start(c, "b8", "D8", "a8.2")
+        start(c, "a0.3", "V0.3", "a8.2")
+        t = near_first(c, [("U0.2", "a0.1"), ("V0.2", "a4.1")], {"a0.1": 0, "a4.1": 4})
+        start(c, "a0.2", t[0][0], t[0][1])
+        finish(c, "a0.2", t[1][0], t[1][1])
+        finish(c, "a0.3", "U0.3", "a0.2")
+        if q == 0:
+            send_val(c, "a0.3", [rk[1], rk[0]])
+            finish(c, "b2", "E2", "a0.3")
+            send_val(c, "b2", [rk[3]])
+            send_val(c, "b2", [rk[2]])
+        if q == 4:
+            finish(c, "b4", "E4", "a0.3")
+            send_val(c, "b4", [rk[5], rk[4]])
+            finish(c, "b6", "E6", "b4")
+            send_val(c, "b6", [rk[7]])
+            send_val(c, "b6", [rk[6]])
+        if q == 8:
+            finish(c, "b8", "E8", "a0.3")
+            send_val(c, "b8", [rk[9]])
+            store(c, "b8")
+            finish(c, "b10", "E10", "b8")
+            send_val(c, "b10", [rk[11]])
+            send_val(c, "b10", [rk[10]])
+        if q == 12:
+            start(c, "b14", "D14", "a14.0")
+            finish(c, "b8", "E8", "a0.3")
+            finish(c, "b12", "E12", "b8")
+            send_val(c, "b12", [rk[13]])
+            store(c, "b12")
+            finish(c, "b14", "E14", "b12")
+            send_val(c, "b14", [rk[15]])
+            send_val(c, "b14", [rk[14]])
+
+    for r in range(16):
+        c = rk[r]
+        if r % 2:
+            par = "a0.3" if r == 1 else "b%d" % (r - 1)
+            finish(c, "b%d" % r, "E%d" % r, par)
+            store(c, "b%d" % r)
+        elif c != Q.get(r):
+            store(c, "a0.3" if r == 0 else "b%d" % r)
+
+    if sent.get(me, 0):
+        g.wait_ge(T.sem.sent, sent[me])

@@ -2,10 +2,11 @@ from concourse.bass import DstId, RemoteDMATransfer
 from concourse.mybir import AluOpType
 
 TK = 512
+HW = TK // 2
 NP = 2
-PW = TK // NP
+PW = HW // NP
 POOL = 12288
-NM, NL = 44, 52
+NM, NL = 40, 72
 
 SCRATCH = {
     "pool": ("sbuf", [128, POOL], "bfloat16"),
@@ -16,20 +17,11 @@ for _b in range(8):
 SEMAPHORES = ["m%d" % i for i in range(NM)] + ["l%d" % i for i in range(NL)] + ["sent"]
 
 
-def _bits(m):
-    n = 0
-    while m:
-        n += m & 1
-        m >>= 1
-    return n
-
-
 def rank_program(g, core, T, topo):
     me = core
     rk = list(T.cores)
     queues = {"g": g, "t": g.tensor, "v": g.vector, "s": g.sync, "a": g.scalar}
-    nmsg = [0]
-    nloc, ncol, waited, sent, banks, where, zcond = {}, {}, {}, {}, {}, {}, {}
+    nmsg, nloc, ncol, waited, sent, banks, where, zcond = {}, {}, {}, {}, {}, {}, {}, {}
     seq = [0]
 
     def lsem(c):
@@ -68,66 +60,94 @@ def rank_program(g, core, T, topo):
                     out.append(cd)
         return out
 
-    def load(c, q, off, tensor, a, b):
+    def load(c, q, spec, tensor, a):
         s = lsem(c)
+        off = where[(c, spec[0][0])][0]
+        w = sum(x[1] for x in spec)
         if c == me:
-            queues[q].dma_start(T.pool[:, off:off + b - a], T[tensor][:, a:b]).then_inc(T.sem[s], 16)
-        return (s, 16)
+            queues[q].dma_start(T.pool[:, off:off + w], T[tensor][:, a:a + w]).then_inc(T.sem[s], 16)
+        regs(c, off, [(s, 16)], spec)
 
-    def send(src, off, w, conds, dsts):
-        s = "m%d" % nmsg[0]
-        nmsg[0] += 1
-        assert nmsg[0] <= NM
+    def layout(c, spec):
+        regs(c, alloc(c, sum(x[1] for x in spec)), [], spec)
+
+    def send(src, w, conds, items):
         wait(src, "g", conds)
-        near = [d for d in dsts if topo.chip(d) == topo.chip(src)]
-        far = [d for d in dsts if topo.chip(d) != topo.chip(src)]
-        groups = []
-        mfar = 0
-        if far:
-            mfar = topo.mask(src, far[0])
-            for d in far:
-                mfar &= topo.mask(src, d)
-            groups.append((far, mfar))
-        if near:
-            mnear = topo.mask(src, near[0])
-            for d in near:
-                mnear &= topo.mask(src, d)
-            groups.append((near, mnear & ~mfar))
-        out = {}
-        trs = []
-        for ds, m in groups:
-            n = _bits(m)
-            assert n in (1, 2, 4, 8, 16)
-            sent[src] = sent.get(src, 0) + n
-            ids, aps = [], []
-            for d in ds:
-                assert topo.may_write(src, d) and d != src
-                o = alloc(d, w)
-                out[d] = (o, (s, n))
-                rid, pid, _se = topo.addr(d)
-                ids.append((rid, pid))
-                aps.append(o)
-            trs.append((ids, aps, m))
+        fars, nears = [], []
+        for i, (off, dsts) in enumerate(items):
+            f = [d for d in dsts if topo.chip(d) != topo.chip(src)]
+            n = [d for d in dsts if topo.chip(d) == topo.chip(src)]
+            if f:
+                fars.append((i, off, f))
+            if n:
+                nears.append((i, off, n))
+        mfar, mnear = 0, 0
+        if fars:
+            mfar = topo.mask(src, fars[0][2][0])
+            for _i, _o, ds in fars:
+                for d in ds:
+                    mfar &= topo.mask(src, d)
+        if nears:
+            mnear = topo.mask(src, nears[0][2][0])
+            for _i, _o, ds in nears:
+                for d in ds:
+                    mnear &= topo.mask(src, d)
+            mnear &= ~mfar
+        out, trs = {}, []
+        for group, m in ((fars, mfar), (nears, mnear)):
+            if not group:
+                continue
+            bits = [b for b in range(m.bit_length()) if (m >> b) & 1]
+            per = len(bits) // len(group)
+            assert per * len(group) == len(bits) and per in (1, 2, 4, 8, 16)
+            for j, (i, off, ds) in enumerate(group):
+                em = sum(1 << b for b in bits[j * per:(j + 1) * per])
+                k = max(nmsg.get(d, 0) for d in ds)
+                assert k < NM
+                s = "m%d" % k
+                sent[src] = sent.get(src, 0) + per
+                ids, aps = [], []
+                for d in ds:
+                    assert topo.may_write(src, d) and d != src
+                    nmsg[d] = k + 1
+                    o = alloc(d, w)
+                    out[(i, d)] = (o, (s, per))
+                    rid, pid, _se = topo.addr(d)
+                    ids.append((rid, pid))
+                    aps.append(o)
+                trs.append((off, ids, aps, em, s))
         if src == me:
-            sap = T.pool[:, off:off + w]
-            if len(trs) == 1 and len(trs[0][0]) == 1:
-                (ids, aps, m) = trs[0]
-                g.remote_dma(out_ap=T.pool[:, aps[0]:aps[0] + w], in_ap=sap, remote_sem=T.sem[s],
-                             local_sem=T.sem.sent, pid=ids[0][1], routing_id=ids[0][0], dma_engine_mask=m)
+            if len(trs) == 1 and len(trs[0][1]) == 1:
+                (off, ids, aps, em, s) = trs[0]
+                g.remote_dma(out_ap=T.pool[:, aps[0]:aps[0] + w], in_ap=T.pool[:, off:off + w], remote_sem=T.sem[s],
+                             local_sem=T.sem.sent, pid=ids[0][1], routing_id=ids[0][0], dma_engine_mask=em)
             else:
                 g.remote_dma_fused(
-                    [RemoteDMATransfer(dst_ids=[DstId(rid=r, pnc=p) for r, p in ids], dma_engine_mask=m,
-                                       remote_sem=T.sem[s], srcs=[sap],
+                    [RemoteDMATransfer(dst_ids=[DstId(rid=r, pnc=p) for r, p in ids], dma_engine_mask=em,
+                                       remote_sem=T.sem[s], srcs=[T.pool[:, off:off + w]],
                                        dsts=[T.pool[:, o:o + w] for o in aps], alu_op=0)
-                     for ids, aps, m in trs],
+                     for off, ids, aps, em, s in trs],
                     local_sem=T.sem.sent)
         return out
 
-    def send_val(src, name, dsts):
-        off, w, _c = where[(src, name)]
-        res = send(src, off, w, allconds(src, name), dsts)
-        for d in dsts:
-            reg(d, name, res[d][0], w, [res[d][1]])
+    def ship(src, blocks):
+        conds, items = [], []
+        w = sum(x[1] for x in blocks[0][0])
+        for spec, dsts in blocks:
+            off = where[(src, spec[0][0])][0]
+            o = off
+            for name, nw in spec:
+                assert where[(src, name)][0] == o
+                o += nw
+                for cd in allconds(src, name):
+                    if cd not in conds:
+                        conds.append(cd)
+            assert o - off == w
+            items.append((off, dsts))
+        res = send(src, w, conds, items)
+        for i, (spec, dsts) in enumerate(blocks):
+            for d in dsts:
+                regs(d, res[(i, d)][0], [res[(i, d)][1]], spec)
 
     def zeros(c):
         if c not in zcond:
@@ -146,7 +166,7 @@ def rank_program(g, core, T, topo):
         conds = list(tc[p]) + list(oc[p])
         if first:
             if (c, node) not in open_nodes:
-                open_nodes[(c, node)] = {"off": alloc(c, TK), "bank": [None] * NP, "conds": [None] * NP}
+                open_nodes[(c, node)] = {"off": alloc(c, HW), "bank": [None] * NP, "conds": [None] * NP}
             free = [b for b in range(8) if bl[b] is None]
             if free:
                 b = free[0]
@@ -177,7 +197,7 @@ def rank_program(g, core, T, topo):
             bl[b] = [seq[0], (rs, 1)]
             nd["conds"][p] = [(rs, 1)]
             if all(x is not None for x in nd["conds"]):
-                where[(c, node)] = (nd["off"], TK, nd["conds"])
+                where[(c, node)] = (nd["off"], HW, nd["conds"])
 
     def start(c, node, tile, opnd):
         for p in range(NP):
@@ -187,42 +207,32 @@ def rank_program(g, core, T, topo):
         for p in range(NP):
             mm(c, node, p, tile, opnd, False, True)
 
-    def store(c, name):
-        off, _w, pc = where[(c, name)]
-        if all(x == pc[0] for x in pc):
-            parts = [("s", 0, TK, pc[0])]
-        else:
-            parts = [("sa"[p % 2], p * PW, (p + 1) * PW, pc[p]) for p in range(NP)]
-        for q, a, b, conds in parts:
-            wait(c, q, conds)
-            s = lsem(c)
-            if c == me:
-                queues[q].dma_start(T.y[:, a:b], T.pool[:, off + a:off + b]).then_inc(T.sem[s], 16)
-            wait(c, q, [(s, 16)])
+    def store(c, name, h):
+        off = where[(c, name)][0]
+        q = "sa"[h]
+        wait(c, q, allconds(c, name))
+        s = lsem(c)
+        if c == me:
+            queues[q].dma_start(T.y[:, h * HW:(h + 1) * HW], T.pool[:, off:off + HW]).then_inc(T.sem[s], 16)
+        wait(c, q, [(s, 16)])
 
     def reaches_all(c):
         return all(topo.may_write(c, d) for d in rk if d != c)
 
     allcores = range(topo.CHIPS * topo.CORES_PER_CHIP)
 
-    def centre_of(r):
-        c = rk[r]
-        if reaches_all(c):
-            return c
-        for h in allcores:
-            if topo.chip(h) == topo.chip(c) and topo.die(h) == topo.die(c) and h not in rk and reaches_all(h):
-                return h
-        raise ValueError("no centre")
+    Q = {}
+    for q in (0, 4, 8, 12):
+        c = rk[q]
+        cand = [c] if reaches_all(c) else []
+        cand += [h for h in allcores if topo.chip(h) == topo.chip(c) and topo.die(h) == topo.die(c)
+                 and h not in rk and reaches_all(h)]
+        Q[(q, 0)], Q[(q, 1)] = cand[0], cand[1]
 
-    Q = {q: centre_of(q) for q in (0, 4, 8, 12)}
-
-    def relay_for(c, dst):
+    def relay_for(c, dsts):
         for h in rk:
-            if h != c and topo.chip(h) == topo.chip(c) and h not in Q.values() and topo.may_write(h, dst):
-                return h
-        for h in allcores:
-            if h != c and topo.chip(h) == topo.chip(c) and h not in rk and h not in Q.values() \
-                    and topo.may_write(h, dst):
+            if h != c and topo.chip(h) == topo.chip(c) and h not in Q.values() \
+                    and all(topo.may_write(h, d) for d in dsts):
                 return h
         raise ValueError("no relay")
 
@@ -235,151 +245,182 @@ def rank_program(g, core, T, topo):
     def de(r):
         return [("D%d" % r, 128), ("E%d" % r, 128)]
 
+    def xh(r, h):
+        return [("x%d#%d" % (r, h), HW)]
+
+    def val(name, h):
+        return [("%s#%d" % (name, h), HW)]
+
+    top0 = uv(0, [2, 3])
+    top8 = uv(8, [2]) + de(8)
+
     relays = []
-
-    def to_centre(c, dst, off, w, conds, spec):
-        if c == dst:
-            regs(c, off, conds, spec)
-        elif topo.may_write(c, dst):
-            o, cd = send(c, off, w, conds, [dst])[dst]
-            regs(dst, o, [cd], spec)
-        else:
-            h = relay_for(c, dst)
-            o, cd = send(c, off, w, conds, [h])[h]
-            relays.append((h, dst, o, w, cd, spec))
-
-    top = {}
     for r in (8, 12, 9, 10, 11, 13, 14, 15, 0, 4, 1, 2, 3, 5, 6, 7):
         c = rk[r]
         q = r - r % 4
+        c0, c1 = Q[(q, 0)], Q[(q, 1)]
         if r % 2:
-            ox, ow = alloc(c, TK), alloc(c, 256)
-            cx = load(c, "s", ox, "x", 0, TK)
-            cw = load(c, "a", ow, "wd", 0, 256)
-            reg(c, "x%d" % r, ox, TK, [cx])
-            regs(c, ow, [cw], de(r))
-            to_centre(c, Q[q], ox, TK, [cx], [("x%d" % r, TK)])
-            start(c, "b%d" % r, "D%d" % r, "x%d" % r)
+            layout(c, xh(r, 0) + xh(r, 1))
+            layout(c, de(r))
+            load(c, "s", xh(r, 0) + xh(r, 1), "x", 0)
+            load(c, "a", de(r), "wd", 0)
+            if topo.may_write(c, c0) and topo.may_write(c, c1):
+                ship(c, [(xh(r, 0), [c0]), (xh(r, 1), [c1])])
+            else:
+                h = relay_for(c, [c0, c1])
+                ship(c, [(xh(r, 0) + xh(r, 1), [h])])
+                relays.append((h, r, c0, c1))
+            for h in range(2):
+                start(c, "b%d#%d" % (r, h), "D%d" % r, "x%d#%d" % (r, h))
         elif r % 4:
-            o = alloc(c, TK + 512)
-            cs = [load(c, "s", o, "x", 0, TK), load(c, "a", o + TK, "wu", 0, 256),
-                  load(c, "a", o + TK + 256, "wd", 0, 256)]
-            to_centre(c, Q[q], o, TK + 512, cs, [("x%d" % r, TK)] + uv(r, [0]) + de(r))
+            layout(c, xh(r, 0) + uv(r, [0]) + xh(r, 1))
+            layout(c, de(r))
+            load(c, "s", xh(r, 0), "x", 0)
+            load(c, "a", uv(r, [0]), "wu", 0)
+            load(c, "s", xh(r, 1), "x", HW)
+            load(c, "a", de(r), "wd", 0)
+            ship(c, [(xh(r, 0) + uv(r, [0]), [c0]), (uv(r, [0]) + xh(r, 1), [c1])])
+            ship(c, [(de(r), [c0]), (de(r), [c1])])
         else:
             if r == 0:
-                o = alloc(c, 512)
-                cs = [load(c, "s", o, "wu", 512, 1024)]
-                top[0] = (o, 512, cs, uv(0, [2, 3]))
-                to_centre(c, Q[0], o, 512, cs, uv(0, [2, 3]))
+                layout(c, top0)
+                load(c, "s", top0, "wu", 512)
+                ship(c, [(top0, [d]) for d in (c0, c1) if d != c])
             if r == 8:
-                o = alloc(c, 512)
-                cs = [load(c, "s", o, "wu", 512, 768), load(c, "a", o + 256, "wd", 0, 256)]
-                to_centre(c, Q[8], o, 512, cs, uv(8, [2]) + de(8))
-            spec = [("x%d" % r, TK)] + uv(r, [0, 1])
-            w = TK + 512
-            o = alloc(c, w + (256 if r % 8 else 0))
-            cs = [load(c, "a" if r == 0 else "s", o, "x", 0, TK), load(c, "s" if r == 0 else "a", o + TK, "wu", 0, 512)]
-            if r % 8:
-                cs.append(load(c, "s", o + w, "wd", 0, 256))
-                spec += de(r)
-                w += 256
-            to_centre(c, Q[q], o, w, cs, spec)
+                layout(c, top8)
+                load(c, "s", uv(8, [2]), "wu", 512)
+                load(c, "a", de(8), "wd", 0)
+                if c != c0:
+                    ship(c, [(top8, [c0])])
+                ship(c0, [(top8, [Q[(12, 1)], c1])])
+            if c != c0 and r % 8:
+                layout(c, uv(r, [1]) + xh(r, 0) + uv(r, [0]) + xh(r, 1) + de(r))
+                load(c, "s", xh(r, 0), "x", 0)
+                load(c, "a", xh(r, 1), "x", HW)
+                load(c, "s", uv(r, [0]), "wu", 0)
+                load(c, "a", uv(r, [1]), "wu", 256)
+                load(c, "s", de(r), "wd", 0)
+                ship(c, [(uv(r, [1]) + xh(r, 0) + uv(r, [0]), [c0]), (uv(r, [0]) + xh(r, 1) + de(r), [c1])])
+                ship(c0, [(uv(r, [1]), [c1])])
+                ship(c1, [(de(r), [c0])])
+            else:
+                w = uv(r, [0, 1]) + (de(r) if r % 8 else [])
+                layout(c, xh(r, 0) + w + xh(r, 1))
+                load(c, "a", xh(r, 0), "x", 0)
+                load(c, "s", uv(r, [0, 1]), "wu", 0)
+                load(c, "a", xh(r, 1), "x", HW)
+                if r % 8:
+                    load(c, "s", de(r), "wd", 0)
+                if c == c0:
+                    ship(c, [(w + xh(r, 1), [c1])])
+                else:
+                    ship(c, [(xh(r, 0) + w, [c0]), (w + xh(r, 1), [c1])])
 
-    for h, dst, o, w, cd, spec in relays:
-        o2, cd2 = send(h, o, w, [cd], [dst])[dst]
-        regs(dst, o2, [cd2], spec)
+    for h, r, c0, c1 in relays:
+        ship(h, [(xh(r, 0), [c0]), (xh(r, 1), [c1])])
 
-    def spread(src, first_tile, spec, dsts):
-        off = where[(src, first_tile)][0]
-        w = sum(x[1] for x in spec)
-        res = send(src, off, w, allconds(src, first_tile), dsts)
-        for d in dsts:
-            regs(d, res[d][0], [res[d][1]], spec)
-
-    spec8 = uv(8, [2]) + de(8)
-    spread(Q[8], "U8.2", spec8, [Q[0], Q[4]])
-    spread(Q[4], "U8.2", spec8, [Q[12]])
-    spread(Q[0], "U0.2", uv(0, [2, 3]), [Q[8], Q[12], Q[4]])
-
-    for q in (8, 12, 0, 4):
-        c = Q[q]
-        a0, a2, a1 = "a%d.0" % q, "a%d.0" % (q + 2), "a%d.1" % q
-        start(c, a0, "U%d.0" % q, "x%d" % q)
-        start(c, a2, "U%d.0" % (q + 2), "x%d" % (q + 2))
-        finish(c, a0, "V%d.0" % q, "x%d" % (q + 1))
-        start(c, a1, "U%d.1" % q, a0)
-        finish(c, a2, "V%d.0" % (q + 2), "x%d" % (q + 3))
-        finish(c, a1, "V%d.1" % q, a2)
-        others = [Q[o] for o in (12, 8, 4, 0) if o != q]
-        near = [d for d in others if topo.chip(d) == topo.chip(c)]
-        far = [d for d in others if topo.chip(d) != topo.chip(c)]
-        if q >= 8:
-            send_val(c, a1, near + far)
-        else:
-            send_val(c, a1, near + far[:1])
-            for d in far[1:]:
-                send_val(c, a1, [d])
-
-    def near_first(c, terms, src):
-        return sorted(terms, key=lambda t: 0 if topo.chip(Q[src[t[1]]]) == topo.chip(c) else 1)
+    for h in range(2):
+        ship(Q[(0, h)], [(top0, [Q[(12, h)], Q[(4, h)], Q[(8, h)]])])
+    ship(Q[(8, 1)], [(top8, [Q[(0, 0)]]), (top8, [Q[(0, 1)]])])
+    ship(Q[(12, 1)], [(top8, [Q[(12, 0)], Q[(4, 0)], Q[(4, 1)]])])
 
     for q in (8, 12, 0, 4):
-        c = Q[q]
-        if q == 0:
-            start(c, "b2", "D2", "a2.0")
-        if q == 4:
-            start(c, "b4", "D4", "a4.1")
-            start(c, "b6", "D6", "a6.0")
-        if q == 8:
-            start(c, "b10", "D10", "a10.0")
-        if q == 12:
-            start(c, "b12", "D12", "a12.1")
-        t = near_first(c, [("U8.2", "a8.1"), ("V8.2", "a12.1")], {"a8.1": 8, "a12.1": 12})
-        start(c, "a8.2", t[0][0], t[0][1])
-        finish(c, "a8.2", t[1][0], t[1][1])
-        if q >= 8:
-            start(c, "b8", "D8", "a8.2")
-        start(c, "a0.3", "V0.3", "a8.2")
-        t = near_first(c, [("U0.2", "a0.1"), ("V0.2", "a4.1")], {"a0.1": 0, "a4.1": 4})
-        start(c, "a0.2", t[0][0], t[0][1])
-        finish(c, "a0.2", t[1][0], t[1][1])
-        finish(c, "a0.3", "U0.3", "a0.2")
-        if q == 0:
-            send_val(c, "a0.3", [rk[1], rk[0]])
-            finish(c, "b2", "E2", "a0.3")
-            send_val(c, "b2", [rk[3]])
-            send_val(c, "b2", [rk[2]])
-        if q == 4:
-            finish(c, "b4", "E4", "a0.3")
-            send_val(c, "b4", [rk[5], rk[4]])
-            finish(c, "b6", "E6", "b4")
-            send_val(c, "b6", [rk[7]])
-            send_val(c, "b6", [rk[6]])
-        if q == 8:
-            finish(c, "b8", "E8", "a0.3")
-            send_val(c, "b8", [rk[9]])
-            store(c, "b8")
-            finish(c, "b10", "E10", "b8")
-            send_val(c, "b10", [rk[11]])
-            send_val(c, "b10", [rk[10]])
-        if q == 12:
-            start(c, "b14", "D14", "a14.0")
-            finish(c, "b8", "E8", "a0.3")
-            finish(c, "b12", "E12", "b8")
-            send_val(c, "b12", [rk[13]])
-            store(c, "b12")
-            finish(c, "b14", "E14", "b12")
-            send_val(c, "b14", [rk[15]])
-            send_val(c, "b14", [rk[14]])
+        for h in range(2):
+            c = Q[(q, h)]
+            sfx = "#%d" % h
+            a0, a2, a1 = "a%d.0" % q + sfx, "a%d.0" % (q + 2) + sfx, "a%d.1" % q + sfx
+            start(c, a0, "U%d.0" % q, "x%d" % q + sfx)
+            start(c, a2, "U%d.0" % (q + 2), "x%d" % (q + 2) + sfx)
+            finish(c, a0, "V%d.0" % q, "x%d" % (q + 1) + sfx)
+            start(c, a1, "U%d.1" % q, a0)
+            finish(c, a2, "V%d.0" % (q + 2), "x%d" % (q + 3) + sfx)
+            finish(c, a1, "V%d.1" % q, a2)
+            others = [Q[(o, h)] for o in (12, 8, 4, 0) if o != q]
+            near = [d for d in others if topo.chip(d) == topo.chip(c)]
+            far = [d for d in others if topo.chip(d) != topo.chip(c)]
+            if q >= 8:
+                ship(c, [([(a1, HW)], near + far)])
+            else:
+                ship(c, [([(a1, HW)], near + far[:1])])
+                for d in far[1:]:
+                    ship(c, [([(a1, HW)], [d])])
+
+    for q in (8, 12, 0, 4):
+        for h in range(2):
+            c = Q[(q, h)]
+            sfx = "#%d" % h
+
+            def S(node, tile, opnd):
+                start(c, node + sfx, tile, opnd + sfx)
+
+            def F(node, tile, opnd):
+                finish(c, node + sfx, tile, opnd + sfx)
+
+            def out(name, ranks):
+                ds = [rk[r] for r in ranks if rk[r] != c]
+                if ds:
+                    ship(c, [(val(name, h), ds)])
+                if len(ds) < len(ranks):
+                    store(c, name + sfx, h)
+
+            def near_first(terms, src):
+                return sorted(terms, key=lambda t: 0 if topo.chip(Q[(src[t[1]], h)]) == topo.chip(c) else 1)
+
+            if q == 0:
+                S("b2", "D2", "a2.0")
+            if q == 4:
+                S("b4", "D4", "a4.1")
+                S("b6", "D6", "a6.0")
+            if q == 8:
+                S("b10", "D10", "a10.0")
+            if q == 12:
+                S("b12", "D12", "a12.1")
+            t = near_first([("U8.2", "a8.1"), ("V8.2", "a12.1")], {"a8.1": 8, "a12.1": 12})
+            S("a8.2", t[0][0], t[0][1])
+            F("a8.2", t[1][0], t[1][1])
+            if q >= 8:
+                S("b8", "D8", "a8.2")
+            S("a0.3", "V0.3", "a8.2")
+            t = near_first([("U0.2", "a0.1"), ("V0.2", "a4.1")], {"a0.1": 0, "a4.1": 4})
+            S("a0.2", t[0][0], t[0][1])
+            F("a0.2", t[1][0], t[1][1])
+            F("a0.3", "U0.3", "a0.2")
+            if q == 0:
+                out("a0.3", [1, 0])
+                F("b2", "E2", "a0.3")
+                out("b2", [3])
+                out("b2", [2])
+            if q == 4:
+                F("b4", "E4", "a0.3")
+                out("b4", [5, 4])
+                F("b6", "E6", "b4")
+                out("b6", [7])
+                out("b6", [6])
+            if q == 8:
+                F("b8", "E8", "a0.3")
+                out("b8", [9, 8])
+                F("b10", "E10", "b8")
+                out("b10", [11])
+                out("b10", [10])
+            if q == 12:
+                S("b14", "D14", "a14.0")
+                F("b8", "E8", "a0.3")
+                F("b12", "E12", "b8")
+                out("b12", [13, 12])
+                F("b14", "E14", "b12")
+                out("b14", [15])
+                out("b14", [14])
 
     for r in range(16):
         c = rk[r]
-        if r % 2:
-            par = "a0.3" if r == 1 else "b%d" % (r - 1)
-            finish(c, "b%d" % r, "E%d" % r, par)
-            store(c, "b%d" % r)
-        elif c != Q.get(r):
-            store(c, "a0.3" if r == 0 else "b%d" % r)
+        for h in range(2):
+            sfx = "#%d" % h
+            if r % 2:
+                par = "a0.3" if r == 1 else "b%d" % (r - 1)
+                finish(c, "b%d" % r + sfx, "E%d" % r, par + sfx)
+                store(c, "b%d" % r + sfx, h)
+            elif c != Q.get((r, h)):
+                store(c, ("a0.3" if r == 0 else "b%d" % r) + sfx, h)
 
     if sent.get(me, 0):
         g.wait_ge(T.sem.sent, sent[me])

@@ -229,6 +229,10 @@ def rank_program(g, core, T, topo):
                  and h not in rk and reaches_all(h)]
         Q[(q, 0)], Q[(q, 1)] = cand[0], cand[1]
 
+    own = [r for r in range(2, 16, 4)
+           if topo.may_write(rk[r], rk[r + 1]) and topo.may_write(rk[r + 1], rk[r])
+           and all(topo.may_write(rk[r], Q[(r - 2, h)]) for h in range(2))]
+
     def relay_for(c, dsts):
         for h in rk:
             if h != c and topo.chip(h) == topo.chip(c) and h not in Q.values() \
@@ -264,7 +268,16 @@ def rank_program(g, core, T, topo):
             layout(c, de(r))
             load(c, "s", xh(r, 0) + xh(r, 1), "x", 0)
             load(c, "a", de(r), "wd", 0)
-            if topo.may_write(c, c0) and topo.may_write(c, c1):
+            if r - 1 in own:
+                e, a = rk[r - 1], "a%d.0" % (r - 1)
+                ship(c, [(xh(r, 0) + xh(r, 1), [e])])
+                for h in range(2):
+                    finish(e, a + "#%d" % h, "V%d.0" % (r - 1), "x%d#%d" % (r, h))
+                    ship(e, [(val(a, h), [Q[(q, h)]])])
+                ship(e, [(val(a, 0), [c]), (val(a, 1), [c])])
+                for h in range(2):
+                    start(e, "b%d#%d" % (r - 1, h), "D%d" % (r - 1), a + "#%d" % h)
+            elif topo.may_write(c, c0) and topo.may_write(c, c1):
                 ship(c, [(xh(r, 0), [c0]), (xh(r, 1), [c1])])
             else:
                 h = relay_for(c, [c0, c1])
@@ -272,6 +285,19 @@ def rank_program(g, core, T, topo):
                 relays.append((h, r, c0, c1))
             for h in range(2):
                 start(c, "b%d#%d" % (r, h), "D%d" % r, "x%d#%d" % (r, h))
+            if r - 1 in own:
+                for h in range(2):
+                    start(c, "b%d#%d" % (r - 1, h), "D%d" % (r - 1), "a%d.0#%d" % (r - 1, h))
+        elif r in own:
+            layout(c, xh(r, 0) + xh(r, 1))
+            layout(c, uv(r, [0]))
+            layout(c, de(r))
+            load(c, "a", de(r), "wd", 0)
+            load(c, "s", xh(r, 0) + xh(r, 1), "x", 0)
+            load(c, "a", uv(r, [0]), "wu", 0)
+            ship(c, [(de(r), [rk[r + 1]])])
+            for h in range(2):
+                start(c, "a%d.0#%d" % (r, h), "U%d.0" % r, "x%d#%d" % (r, h))
         elif r % 4:
             layout(c, xh(r, 0) + uv(r, [0]) + xh(r, 1))
             layout(c, de(r))
@@ -330,10 +356,12 @@ def rank_program(g, core, T, topo):
             sfx = "#%d" % h
             a0, a2, a1 = "a%d.0" % q + sfx, "a%d.0" % (q + 2) + sfx, "a%d.1" % q + sfx
             start(c, a0, "U%d.0" % q, "x%d" % q + sfx)
-            start(c, a2, "U%d.0" % (q + 2), "x%d" % (q + 2) + sfx)
+            if q + 2 not in own:
+                start(c, a2, "U%d.0" % (q + 2), "x%d" % (q + 2) + sfx)
             finish(c, a0, "V%d.0" % q, "x%d" % (q + 1) + sfx)
             start(c, a1, "U%d.1" % q, a0)
-            finish(c, a2, "V%d.0" % (q + 2), "x%d" % (q + 3) + sfx)
+            if q + 2 not in own:
+                finish(c, a2, "V%d.0" % (q + 2), "x%d" % (q + 3) + sfx)
             finish(c, a1, "V%d.1" % q, a2)
             others = [Q[(o, h)] for o in (12, 8, 4, 0) if o != q]
             near = [d for d in others if topo.chip(d) == topo.chip(c)]
@@ -366,15 +394,19 @@ def rank_program(g, core, T, topo):
             def near_first(terms, src):
                 return sorted(terms, key=lambda t: 0 if topo.chip(Q[(src[t[1]], h)]) == topo.chip(c) else 1)
 
-            if q == 0:
-                S("b2", "D2", "a2.0")
-            if q == 4:
-                S("b4", "D4", "a4.1")
-                S("b6", "D6", "a6.0")
-            if q == 8:
-                S("b10", "D10", "a10.0")
-            if q == 12:
-                S("b12", "D12", "a12.1")
+            def down(par):
+                if q + 2 in own:
+                    out(par, [q + 3, q + 2, q + 1, q])
+                else:
+                    out(par, [q + 1, q])
+                    F("b%d" % (q + 2), "E%d" % (q + 2), par)
+                    out("b%d" % (q + 2), [q + 3])
+                    out("b%d" % (q + 2), [q + 2])
+
+            if q % 8:
+                S("b%d" % q, "D%d" % q, "a%d.1" % q)
+            if q + 2 not in own and q != 12:
+                S("b%d" % (q + 2), "D%d" % (q + 2), "a%d.0" % (q + 2))
             t = near_first([("U8.2", "a8.1"), ("V8.2", "a12.1")], {"a8.1": 8, "a12.1": 12})
             S("a8.2", t[0][0], t[0][1])
             F("a8.2", t[1][0], t[1][1])
@@ -386,33 +418,32 @@ def rank_program(g, core, T, topo):
             F("a0.2", t[1][0], t[1][1])
             F("a0.3", "U0.3", "a0.2")
             if q == 0:
-                out("a0.3", [1, 0])
-                F("b2", "E2", "a0.3")
-                out("b2", [3])
-                out("b2", [2])
+                down("a0.3")
             if q == 4:
                 F("b4", "E4", "a0.3")
-                out("b4", [5, 4])
-                F("b6", "E6", "b4")
-                out("b6", [7])
-                out("b6", [6])
+                down("b4")
             if q == 8:
                 F("b8", "E8", "a0.3")
-                out("b8", [9, 8])
-                F("b10", "E10", "b8")
-                out("b10", [11])
-                out("b10", [10])
+                down("b8")
             if q == 12:
-                S("b14", "D14", "a14.0")
+                if q + 2 not in own:
+                    S("b14", "D14", "a14.0")
                 F("b8", "E8", "a0.3")
                 F("b12", "E12", "b8")
-                out("b12", [13, 12])
-                F("b14", "E14", "b12")
-                out("b14", [15])
-                out("b14", [14])
+                down("b12")
 
     for r in range(16):
         c = rk[r]
+        q = r - r % 4
+        top = "a0.3" if q == 0 else "b%d" % q
+        if r in own:
+            for h in range(2):
+                finish(c, "b%d#%d" % (r, h), "E%d" % r, "%s#%d" % (top, h))
+                store(c, "b%d#%d" % (r, h), h)
+            continue
+        if r - 1 in own:
+            for h in range(2):
+                finish(c, "b%d#%d" % (r - 1, h), "E%d" % (r - 1), "%s#%d" % (top, h))
         for h in range(2):
             sfx = "#%d" % h
             if r % 2:

from concourse.bass import DstId, RemoteDMATransfer
from concourse.mybir import AluOpType

TK = 512
HW = TK // 2
NP = 2
PW = HW // NP
POOL = 12288
NM, NL = 40, 72

SCRATCH = {
    "pool": ("sbuf", [128, POOL], "bfloat16"),
    "zero": ("sbuf", [128, PW], "float32"),
}
for _b in range(8):
    SCRATCH["ps%d" % _b] = ("psum", [128, 512], "float32")
SEMAPHORES = ["m%d" % i for i in range(NM)] + ["l%d" % i for i in range(NL)] + ["sent"]


def rank_program(g, core, T, topo):
    me = core
    rk = list(T.cores)
    queues = {"g": g, "t": g.tensor, "v": g.vector, "s": g.sync, "a": g.scalar}
    nmsg, nloc, ncol, waited, sent, banks, where, zcond = {}, {}, {}, {}, {}, {}, {}, {}
    seq = [0]

    def lsem(c):
        n = nloc.get(c, 0)
        nloc[c] = n + 1
        assert n < NL
        return "l%d" % n

    def alloc(c, w):
        o = ncol.get(c, 0)
        ncol[c] = o + w
        assert o + w <= POOL
        return o

    def wait(c, q, conds):
        done = waited.setdefault((c, q), set())
        for cd in conds:
            if cd not in done:
                done.add(cd)
                if c == me:
                    queues[q].wait_ge(T.sem[cd[0]], cd[1])

    def reg(c, name, off, w, conds):
        where[(c, name)] = (off, w, [list(conds) for _ in range(NP)])

    def regs(c, off, conds, spec):
        for name, w in spec:
            reg(c, name, off, w, conds)
            off += w

    def allconds(c, name):
        out = []
        for pc in where[(c, name)][2]:
            for cd in pc:
                if cd not in out:
                    out.append(cd)
        return out

    def load(c, q, spec, tensor, a):
        s = lsem(c)
        off = where[(c, spec[0][0])][0]
        w = sum(x[1] for x in spec)
        if c == me:
            queues[q].dma_start(T.pool[:, off:off + w], T[tensor][:, a:a + w]).then_inc(T.sem[s], 16)
        regs(c, off, [(s, 16)], spec)

    def layout(c, spec):
        regs(c, alloc(c, sum(x[1] for x in spec)), [], spec)

    def send(src, w, conds, items):
        wait(src, "g", conds)
        fars, nears = [], []
        for i, (off, dsts) in enumerate(items):
            f = [d for d in dsts if topo.chip(d) != topo.chip(src)]
            n = [d for d in dsts if topo.chip(d) == topo.chip(src)]
            if f:
                fars.append((i, off, f))
            if n:
                nears.append((i, off, n))
        mfar, mnear = 0, 0
        if fars:
            mfar = topo.mask(src, fars[0][2][0])
            for _i, _o, ds in fars:
                for d in ds:
                    mfar &= topo.mask(src, d)
        if nears:
            mnear = topo.mask(src, nears[0][2][0])
            for _i, _o, ds in nears:
                for d in ds:
                    mnear &= topo.mask(src, d)
            mnear &= ~mfar
        out, trs = {}, []
        for group, m in ((fars, mfar), (nears, mnear)):
            if not group:
                continue
            bits = [b for b in range(m.bit_length()) if (m >> b) & 1]
            per = len(bits) // len(group)
            assert per * len(group) == len(bits) and per in (1, 2, 4, 8, 16)
            for j, (i, off, ds) in enumerate(group):
                em = sum(1 << b for b in bits[j * per:(j + 1) * per])
                k = max(nmsg.get(d, 0) for d in ds)
                assert k < NM
                s = "m%d" % k
                sent[src] = sent.get(src, 0) + per
                ids, aps = [], []
                for d in ds:
                    assert topo.may_write(src, d) and d != src
                    nmsg[d] = k + 1
                    o = alloc(d, w)
                    out[(i, d)] = (o, (s, per))
                    rid, pid, _se = topo.addr(d)
                    ids.append((rid, pid))
                    aps.append(o)
                trs.append((off, ids, aps, em, s))
        if src == me:
            if len(trs) == 1 and len(trs[0][1]) == 1:
                (off, ids, aps, em, s) = trs[0]
                g.remote_dma(out_ap=T.pool[:, aps[0]:aps[0] + w], in_ap=T.pool[:, off:off + w], remote_sem=T.sem[s],
                             local_sem=T.sem.sent, pid=ids[0][1], routing_id=ids[0][0], dma_engine_mask=em)
            else:
                g.remote_dma_fused(
                    [RemoteDMATransfer(dst_ids=[DstId(rid=r, pnc=p) for r, p in ids], dma_engine_mask=em,
                                       remote_sem=T.sem[s], srcs=[T.pool[:, off:off + w]],
                                       dsts=[T.pool[:, o:o + w] for o in aps], alu_op=0)
                     for off, ids, aps, em, s in trs],
                    local_sem=T.sem.sent)
        return out

    def ship(src, blocks):
        conds, items = [], []
        w = sum(x[1] for x in blocks[0][0])
        for spec, dsts in blocks:
            off = where[(src, spec[0][0])][0]
            o = off
            for name, nw in spec:
                assert where[(src, name)][0] == o
                o += nw
                for cd in allconds(src, name):
                    if cd not in conds:
                        conds.append(cd)
            assert o - off == w
            items.append((off, dsts))
        res = send(src, w, conds, items)
        for i, (spec, dsts) in enumerate(blocks):
            for d in dsts:
                regs(d, res[(i, d)][0], [res[(i, d)][1]], spec)

    def zeros(c):
        if c not in zcond:
            s = lsem(c)
            zcond[c] = (s, 1)
            if c == me:
                g.vector.memset(T.zero[:], 0.0).then_inc(T.sem[s], 1)

    open_nodes = {}

    def mm(c, node, p, tile, opnd, first, last):
        zeros(c)
        bl = banks.setdefault(c, [None] * 8)
        toff, _tw, tc = where[(c, tile)]
        ooff, _ow, oc = where[(c, opnd)]
        conds = list(tc[p]) + list(oc[p])
        if first:
            if (c, node) not in open_nodes:
                open_nodes[(c, node)] = {"off": alloc(c, HW), "bank": [None] * NP, "conds": [None] * NP}
            free = [b for b in range(8) if bl[b] is None]
            if free:
                b = free[0]
            else:
                closed = [b for b in range(8) if bl[b][1] is not None]
                assert closed, "no PSUM bank free"
                b = min(closed, key=lambda k: bl[k][0])
                conds.append(bl[b][1])
            seq[0] += 1
            bl[b] = [seq[0], None]
            open_nodes[(c, node)]["bank"][p] = b
        nd = open_nodes[(c, node)]
        b = nd["bank"][p]
        wait(c, "t", conds)
        ms = lsem(c) if last else None
        if c == me:
            ins = g.tensor.matmul(T["ps%d" % b][:, 0:PW], T.pool[:, toff:toff + 128],
                                  T.pool[:, ooff + p * PW:ooff + (p + 1) * PW], first, last)
            if last:
                ins.then_inc(T.sem[ms], 1)
        if last:
            rs = lsem(c)
            wait(c, "v", [zcond[c], (ms, 1)])
            if c == me:
                g.vector.tensor_tensor(T.pool[:, nd["off"] + p * PW:nd["off"] + (p + 1) * PW],
                                       T["ps%d" % b][:, 0:PW], T.zero[:, 0:PW], AluOpType.max).then_inc(T.sem[rs], 1)
            seq[0] += 1
            bl[b] = [seq[0], (rs, 1)]
            nd["conds"][p] = [(rs, 1)]
            if all(x is not None for x in nd["conds"]):
                where[(c, node)] = (nd["off"], HW, nd["conds"])

    def start(c, node, tile, opnd):
        for p in range(NP):
            mm(c, node, p, tile, opnd, True, False)

    def finish(c, node, tile, opnd):
        for p in range(NP):
            mm(c, node, p, tile, opnd, False, True)

    def store(c, name, h):
        off = where[(c, name)][0]
        q = "sa"[h]
        wait(c, q, allconds(c, name))
        s = lsem(c)
        if c == me:
            queues[q].dma_start(T.y[:, h * HW:(h + 1) * HW], T.pool[:, off:off + HW]).then_inc(T.sem[s], 16)
        wait(c, q, [(s, 16)])

    def reaches_all(c):
        return all(topo.may_write(c, d) for d in rk if d != c)

    allcores = range(topo.CHIPS * topo.CORES_PER_CHIP)

    Q = {}
    for q in (0, 4, 8, 12):
        c = rk[q]
        cand = [c] if reaches_all(c) else []
        cand += [h for h in allcores if topo.chip(h) == topo.chip(c) and topo.die(h) == topo.die(c)
                 and h not in rk and reaches_all(h)]
        Q[(q, 0)], Q[(q, 1)] = cand[0], cand[1]

    own = [r for r in range(2, 16, 4)
           if topo.may_write(rk[r], rk[r + 1]) and topo.may_write(rk[r + 1], rk[r])
           and all(topo.may_write(rk[r], Q[(r - 2, h)]) for h in range(2))]

    def relay_for(c, dsts):
        for h in rk:
            if h != c and topo.chip(h) == topo.chip(c) and h not in Q.values() \
                    and all(topo.may_write(h, d) for d in dsts):
                return h
        raise ValueError("no relay")

    def uv(r, levels):
        out = []
        for l in levels:
            out += [("U%d.%d" % (r, l), 128), ("V%d.%d" % (r, l), 128)]
        return out

    def de(r):
        return [("D%d" % r, 128), ("E%d" % r, 128)]

    def xh(r, h):
        return [("x%d#%d" % (r, h), HW)]

    def val(name, h):
        return [("%s#%d" % (name, h), HW)]

    top0 = uv(0, [2, 3])
    top8 = uv(8, [2]) + de(8)

    relays = []
    for r in (8, 12, 9, 10, 11, 13, 14, 15, 0, 4, 1, 2, 3, 5, 6, 7):
        c = rk[r]
        q = r - r % 4
        c0, c1 = Q[(q, 0)], Q[(q, 1)]
        if r % 2:
            layout(c, xh(r, 0) + xh(r, 1))
            layout(c, de(r))
            load(c, "s", xh(r, 0) + xh(r, 1), "x", 0)
            load(c, "a", de(r), "wd", 0)
            if r - 1 in own:
                e, a = rk[r - 1], "a%d.0" % (r - 1)
                ship(c, [(xh(r, 0) + xh(r, 1), [e])])
                for h in range(2):
                    finish(e, a + "#%d" % h, "V%d.0" % (r - 1), "x%d#%d" % (r, h))
                    ship(e, [(val(a, h), [Q[(q, h)]])])
                ship(e, [(val(a, 0), [c]), (val(a, 1), [c])])
                for h in range(2):
                    start(e, "b%d#%d" % (r - 1, h), "D%d" % (r - 1), a + "#%d" % h)
            elif topo.may_write(c, c0) and topo.may_write(c, c1):
                ship(c, [(xh(r, 0), [c0]), (xh(r, 1), [c1])])
            else:
                h = relay_for(c, [c0, c1])
                ship(c, [(xh(r, 0) + xh(r, 1), [h])])
                relays.append((h, r, c0, c1))
            for h in range(2):
                start(c, "b%d#%d" % (r, h), "D%d" % r, "x%d#%d" % (r, h))
            if r - 1 in own:
                for h in range(2):
                    start(c, "b%d#%d" % (r - 1, h), "D%d" % (r - 1), "a%d.0#%d" % (r - 1, h))
        elif r in own:
            layout(c, xh(r, 0) + xh(r, 1))
            layout(c, uv(r, [0]))
            layout(c, de(r))
            load(c, "a", de(r), "wd", 0)
            load(c, "s", xh(r, 0) + xh(r, 1), "x", 0)
            load(c, "a", uv(r, [0]), "wu", 0)
            ship(c, [(de(r), [rk[r + 1]])])
            for h in range(2):
                start(c, "a%d.0#%d" % (r, h), "U%d.0" % r, "x%d#%d" % (r, h))
        elif r % 4:
            layout(c, xh(r, 0) + uv(r, [0]) + xh(r, 1))
            layout(c, de(r))
            load(c, "s", xh(r, 0), "x", 0)
            load(c, "a", uv(r, [0]), "wu", 0)
            load(c, "s", xh(r, 1), "x", HW)
            load(c, "a", de(r), "wd", 0)
            ship(c, [(xh(r, 0) + uv(r, [0]), [c0]), (uv(r, [0]) + xh(r, 1), [c1])])
            ship(c, [(de(r), [c0]), (de(r), [c1])])
        else:
            if r == 0:
                layout(c, top0)
                load(c, "s", top0, "wu", 512)
                ship(c, [(top0, [d]) for d in (c0, c1) if d != c])
            if r == 8:
                layout(c, top8)
                load(c, "s", uv(8, [2]), "wu", 512)
                load(c, "a", de(8), "wd", 0)
                if c != c0:
                    ship(c, [(top8, [c0])])
                ship(c0, [(top8, [Q[(12, 1)], c1])])
            if c != c0 and r % 8:
                layout(c, uv(r, [1]) + xh(r, 0) + uv(r, [0]) + xh(r, 1) + de(r))
                load(c, "s", xh(r, 0), "x", 0)
                load(c, "a", xh(r, 1), "x", HW)
                load(c, "s", uv(r, [0]), "wu", 0)
                load(c, "a", uv(r, [1]), "wu", 256)
                load(c, "s", de(r), "wd", 0)
                ship(c, [(uv(r, [1]) + xh(r, 0) + uv(r, [0]), [c0]), (uv(r, [0]) + xh(r, 1) + de(r), [c1])])
                ship(c0, [(uv(r, [1]), [c1])])
                ship(c1, [(de(r), [c0])])
            else:
                w = uv(r, [0, 1]) + (de(r) if r % 8 else [])
                layout(c, xh(r, 0) + w + xh(r, 1))
                load(c, "a", xh(r, 0), "x", 0)
                load(c, "s", uv(r, [0, 1]), "wu", 0)
                load(c, "a", xh(r, 1), "x", HW)
                if r % 8:
                    load(c, "s", de(r), "wd", 0)
                if c == c0:
                    ship(c, [(w + xh(r, 1), [c1])])
                else:
                    ship(c, [(xh(r, 0) + w, [c0]), (w + xh(r, 1), [c1])])

    for h, r, c0, c1 in relays:
        ship(h, [(xh(r, 0), [c0]), (xh(r, 1), [c1])])

    for h in range(2):
        ship(Q[(0, h)], [(top0, [Q[(12, h)], Q[(4, h)], Q[(8, h)]])])
    ship(Q[(8, 1)], [(top8, [Q[(0, 0)]]), (top8, [Q[(0, 1)]])])
    ship(Q[(12, 1)], [(top8, [Q[(12, 0)], Q[(4, 0)], Q[(4, 1)]])])

    for q in (8, 12, 0, 4):
        for h in range(2):
            c = Q[(q, h)]
            sfx = "#%d" % h
            a0, a2, a1 = "a%d.0" % q + sfx, "a%d.0" % (q + 2) + sfx, "a%d.1" % q + sfx
            start(c, a0, "U%d.0" % q, "x%d" % q + sfx)
            if q + 2 not in own:
                start(c, a2, "U%d.0" % (q + 2), "x%d" % (q + 2) + sfx)
            finish(c, a0, "V%d.0" % q, "x%d" % (q + 1) + sfx)
            start(c, a1, "U%d.1" % q, a0)
            if q + 2 not in own:
                finish(c, a2, "V%d.0" % (q + 2), "x%d" % (q + 3) + sfx)
            finish(c, a1, "V%d.1" % q, a2)
            others = [Q[(o, h)] for o in (12, 8, 4, 0) if o != q]
            near = [d for d in others if topo.chip(d) == topo.chip(c)]
            far = [d for d in others if topo.chip(d) != topo.chip(c)]
            if q >= 8:
                ship(c, [([(a1, HW)], near + far)])
            else:
                ship(c, [([(a1, HW)], near + far[:1])])
                for d in far[1:]:
                    ship(c, [([(a1, HW)], [d])])

    for q in (8, 12, 0, 4):
        for h in range(2):
            c = Q[(q, h)]
            sfx = "#%d" % h

            def S(node, tile, opnd):
                start(c, node + sfx, tile, opnd + sfx)

            def F(node, tile, opnd):
                finish(c, node + sfx, tile, opnd + sfx)

            def out(name, ranks):
                ds = [rk[r] for r in ranks if rk[r] != c]
                if ds:
                    ship(c, [(val(name, h), ds)])
                if len(ds) < len(ranks):
                    store(c, name + sfx, h)

            def near_first(terms, src):
                return sorted(terms, key=lambda t: 0 if topo.chip(Q[(src[t[1]], h)]) == topo.chip(c) else 1)

            def down(par):
                if q + 2 in own:
                    out(par, [q + 3, q + 2, q + 1, q])
                else:
                    out(par, [q + 1, q])
                    F("b%d" % (q + 2), "E%d" % (q + 2), par)
                    out("b%d" % (q + 2), [q + 3])
                    out("b%d" % (q + 2), [q + 2])

            if q % 8:
                S("b%d" % q, "D%d" % q, "a%d.1" % q)
            if q + 2 not in own and q != 12:
                S("b%d" % (q + 2), "D%d" % (q + 2), "a%d.0" % (q + 2))
            t = near_first([("U8.2", "a8.1"), ("V8.2", "a12.1")], {"a8.1": 8, "a12.1": 12})
            S("a8.2", t[0][0], t[0][1])
            F("a8.2", t[1][0], t[1][1])
            if q >= 8:
                S("b8", "D8", "a8.2")
            S("a0.3", "V0.3", "a8.2")
            t = near_first([("U0.2", "a0.1"), ("V0.2", "a4.1")], {"a0.1": 0, "a4.1": 4})
            S("a0.2", t[0][0], t[0][1])
            F("a0.2", t[1][0], t[1][1])
            F("a0.3", "U0.3", "a0.2")
            if q == 0:
                down("a0.3")
            if q == 4:
                F("b4", "E4", "a0.3")
                down("b4")
            if q == 8:
                F("b8", "E8", "a0.3")
                down("b8")
            if q == 12:
                if q + 2 not in own:
                    S("b14", "D14", "a14.0")
                F("b8", "E8", "a0.3")
                F("b12", "E12", "b8")
                down("b12")

    for r in range(16):
        c = rk[r]
        q = r - r % 4
        top = "a0.3" if q == 0 else "b%d" % q
        if r in own:
            for h in range(2):
                finish(c, "b%d#%d" % (r, h), "E%d" % r, "%s#%d" % (top, h))
                store(c, "b%d#%d" % (r, h), h)
            continue
        if r - 1 in own:
            for h in range(2):
                finish(c, "b%d#%d" % (r - 1, h), "E%d" % (r - 1), "%s#%d" % (top, h))
        for h in range(2):
            sfx = "#%d" % h
            if r % 2:
                par = "a0.3" if r == 1 else "b%d" % (r - 1)
                finish(c, "b%d" % r + sfx, "E%d" % r, par + sfx)
                store(c, "b%d" % r + sfx, h)
            elif c != Q.get((r, h)):
                store(c, ("a0.3" if r == 0 else "b%d" % r) + sfx, h)

    if sent.get(me, 0):
        g.wait_ge(T.sem.sent, sent[me])
